import numpy as np, ml_dtypes
CORES = [25,29,65,69,153,157,193,197]
N = 8
DEG, TK = 3, 512
MASK = [[4,6,0],[4,6,1],[4,6,2],[4,6,3],[4,6,0],[4,6,5],[4,6,0],[4,6,7]]
def setup_inputs(rng):
    return {"x": rng.standard_normal((N, 128, TK), dtype=np.float32).astype(ml_dtypes.bfloat16), "w": rng.standard_normal((N, 128, DEG * 128), dtype=np.float32).astype(ml_dtypes.bfloat16)}
def setup_inputs_big(rng):
    d = setup_inputs(rng)
    for k in ("x", "w"): d[k] = (d[k].astype(np.float32) * 1024.0).astype(d[k].dtype)
    return d
def setup_inputs_small(rng):
    d = setup_inputs(rng)
    for k in ("x", "w"): d[k] = (d[k].astype(np.float32) * (1 / 1024.0)).astype(d[k].dtype)
    return d
def setup_inputs_apart(rng):
    d = setup_inputs(rng)
    f = (10.0 ** rng.permutation(np.linspace(-1.5, 1.5, N))).astype(np.float32).reshape(N, 1, 1)
    for k in ("x", "w"): d[k] = (d[k].astype(np.float32) * f).astype(d[k].dtype)
    return d
def reference(x, w):
    X, W = x.astype(np.float64), w.astype(np.float64)
    y = np.zeros((N, 128, TK))
    for r in range(N):
        for i, j in enumerate(MASK[r]):
            y[r] += W[r][:, 128 * i:128 * i + 128].T @ X[j]
    return {"y": y.astype(ml_dtypes.bfloat16 if x.dtype != np.float64 else np.float64)}

@@ -1,0 +1,211 @@
+from concourse.bass import DstId, RemoteDMATransfer
+
+P, TK, DEG = 128, 512, 3
+NH = 2
+HW = TK // NH
+FEED_ENGINES = 4
+OUT_ENGINES = 8
+
+SCRATCH = {
+    "xs": ("sbuf", [P, TK], "bfloat16"),
+    "ws": ("sbuf", [P, DEG * P], "bfloat16"),
+    "land0": ("sbuf", [P, TK], "bfloat16"),
+    "land1": ("sbuf", [P, TK], "bfloat16"),
+    "land2": ("sbuf", [P, TK], "bfloat16"),
+    "ys": ("sbuf", [P, TK], "bfloat16"),
+    "xd": ("dram", [P, TK], "bfloat16"),
+    "rd": ("dram", [P, TK], "bfloat16"),
+    "ps0": ("psum", [P, TK], "float32"),
+    "ps1": ("psum", [P, TK], "float32"),
+}
+SEMAPHORES = ["ldd", "ldx", "ldw", "fed", "sent", "a0", "a1", "a2", "mm0", "mm1", "cp0", "cp1", "st0", "st1"]
+
+_CACHE = {}
+
+
+def _bits(m):
+    return [e for e in range(m.bit_length()) if (m >> e) & 1]
+
+
+def _pow2(n):
+    k = 1
+    while 2 * k <= n:
+        k *= 2
+    return k
+
+
+def _spread(engines, k):
+    k = min(k, len(engines))
+    return engines[::len(engines) // k][:k]
+
+
+def _deal(engines, n, k):
+    used = _spread(engines, n * k)
+    return [sum(1 << e for e in used[t::n]) for t in range(n)]
+
+
+def _make_plan(T, topo):
+    cores, mask = list(T.cores), T.tables["MASK"]
+    n = len(cores)
+    world = range(topo.CORES_PER_HOST * (1 + max(topo.host(c) for c in cores)))
+
+    def where(c):
+        return (topo.host(c), topo.chip(c))
+
+    direct, units = {}, []
+    for j in range(n):
+        for r in range(n):
+            if r != j and j in mask[r]:
+                if topo.may_write(cores[j], cores[r]):
+                    direct.setdefault(j, []).append(r)
+                else:
+                    units.append((j, r))
+
+    owners = []
+    for j, r in units:
+        by_die = {}
+        for c in world:
+            if where(c) == where(cores[j]) and T.rank_of(c) is None and topo.may_write(c, cores[r]):
+                by_die.setdefault(topo.die(c), []).append(c)
+        owners.append(by_die)
+
+    base = {}
+    for j, rs in direct.items():
+        for r in rs:
+            if where(cores[j]) != where(cores[r]):
+                d = topo.die(cores[j])
+                for key in (("out", where(cores[j]), d), ("in", where(cores[r]), d)):
+                    base[key] = base.get(key, 0) + 1
+
+    best, total = None, 1
+    for by_die in owners:
+        total *= len(by_die)
+    for code in range(total):
+        load, count, pick, cross = dict(base), {}, [], 0
+        for (j, r), by_die in zip(units, owners):
+            dies = sorted(by_die)
+            d = dies[code % len(dies)]
+            code //= len(dies)
+            pick.append(d)
+            cross += d != topo.die(cores[j])
+            keys = [("mate", where(cores[j]), d)]
+            if not topo.mates(cores[j], cores[r]):
+                keys.append(("in", where(cores[r]), d))
+            for key in keys:
+                load[key] = load.get(key, 0) + 1
+            key = (j, d, len(by_die[d]))
+            count[key] = count.get(key, 0) + 1
+        busy = list(load.values()) + [-(-v // key[2]) for key, v in count.items()]
+        score = (sorted(busy, reverse=True), cross)
+        if best is None or score < best[0]:
+            best = (score, pick)
+
+    relays, feeds, seen = {}, {}, {}
+    for (j, r), by_die, d in zip(units, owners, best[1] if best else []):
+        k = seen.get((j, d), 0)
+        seen[(j, d)] = k + 1
+        c = by_die[d][k % len(by_die[d])]
+        if c not in relays:
+            relays[c] = {"src": j, "dests": []}
+            feeds.setdefault(j, []).append((k, d != topo.die(cores[j]), c))
+        relays[c]["dests"].append(r)
+    feeds = {j: [c for _, _, c in sorted(v)] for j, v in feeds.items()}
+
+    count, late, calls = {}, {}, {}
+    for j in sorted(set(direct) | set(feeds)):
+        src, first, second = cores[j], [], []
+        hs = feeds.get(j, [])
+        if hs:
+            for c, m in zip(hs, _deal(_bits(topo.mask(src, hs[0])), len(hs), FEED_ENGINES)):
+                first.append((c, m))
+                relays[c]["fed"] = len(_bits(m))
+        away = [r for r in direct.get(j, []) if where(cores[r]) != where(src)]
+        home = [r for r in direct.get(j, []) if where(cores[r]) == where(src)]
+        taken = _bits(topo.mask(src, cores[away[0]])) if away else []
+        for rs, engines, hops in ((away, taken, 2),
+                                  (home, [e for e in _bits(topo.mask(src, cores[home[0]])) if e not in taken] if home else [], 1)):
+            if rs:
+                for r, m in zip(rs, _deal(engines, len(rs), _pow2(len(engines) // len(rs)))):
+                    second.append((r, m))
+                    count[(r, j)], late[(r, j)] = len(_bits(m)), (hops, 0)
+        calls[j] = (first, second)
+    for c, job in relays.items():
+        ds = job["dests"]
+        engines = _bits(topo.mask(c, cores[ds[0]]))
+        job["masks"] = _deal(engines, len(ds), _pow2(min(OUT_ENGINES, len(engines)) // len(ds)))
+        for r, m in zip(ds, job["masks"]):
+            count[(r, job["src"])], late[(r, job["src"])] = len(_bits(m)), (3, len(feeds[job["src"]]))
+    return {"relays": relays, "calls": calls, "count": count, "late": late}
+
+
+def _send(g, core, T, topo, src_ap, items):
+    trs = []
+    for dst, ap, sem, m in items:
+        rid, pid = topo.addr(dst, core)
+        trs.append(RemoteDMATransfer(dst_ids=[DstId(rid=rid, pnc=pid)], dma_engine_mask=m, remote_sem=sem,
+                                     src=src_ap, dst=ap))
+    g.remote_dma_fused(trs, local_sem=T.sem.sent)
+    return sum(len(_bits(m)) for _, _, _, m in items)
+
+
+def rank_program(g, core, T, topo):
+    if "plan" not in _CACHE:
+        _CACHE["plan"] = _make_plan(T, topo)
+    plan = _CACHE["plan"]
+    cores, mask = list(T.cores), T.tables["MASK"]
+    rank = T.rank_of(core)
+
+    def landing(r, j):
+        i = mask[r].index(j)
+        return cores[r], T["land%d" % i][:], T.sem["a%d" % i]
+
+    if rank is None:
+        job = plan["relays"].get(core)
+        if job is None:
+            return
+        g.wait_ge(T.sem.fed, job["fed"])
+        left = _send(g, core, T, topo, T.rd[:], [landing(r, job["src"]) + (m,) for r, m in zip(job["dests"], job["masks"])])
+        g.wait_ge(T.sem.sent, left)
+        return
+
+    source = rank in plan["calls"]
+    if source:
+        g.sync.dma_start(T.xd[:], T.x[:]).then_inc(T.sem.ldd, 16)
+    if rank in mask[rank]:
+        g.sync.dma_start(T.xs[:], T.x[:]).then_inc(T.sem.ldx, 16)
+    (g.sync if source else g.scalar).dma_start(T.ws[:], T.w[:]).then_inc(T.sem.ldw, 16)
+
+    if source:
+        first, second = plan["calls"][rank]
+        g.wait_ge(T.sem.ldd, 16)
+        left = 0
+        if first:
+            left += _send(g, core, T, topo, T.xd[:], [(c, T.rd[:], T.sem.fed, m) for c, m in first])
+        if second:
+            left += _send(g, core, T, topo, T.xd[:], [landing(r, rank) + (m,) for r, m in second])
+        g.wait_ge(T.sem.sent, left)
+
+    te = g.tensor
+    te.wait_ge(T.sem.ldw, 16)
+    order = sorted(range(DEG), key=lambda i: plan["late"].get((rank, mask[rank][i]), (0, 0)))
+    for k, i in enumerate(order):
+        j = mask[rank][i]
+        if j == rank:
+            te.wait_ge(T.sem.ldx, 16)
+            buf = T.xs
+        else:
+            _, _, sem = landing(rank, j)
+            te.wait_ge(sem, plan["count"][(rank, j)])
+            buf = T["land%d" % mask[rank].index(j)]
+        for h in range(NH):
+            mm = te.matmul(T["ps%d" % h][:, 0:HW], T.ws[:, P * i:P * (i + 1)], buf[:, HW * h:HW * (h + 1)],
+                           k == 0, k == DEG - 1)
+            if k == DEG - 1:
+                mm.then_inc(T.sem["mm%d" % h], 1)
+
+    for h, q in zip(range(NH), (g.sync, g.scalar)):
+        g.vector.wait_ge(T.sem["mm%d" % h], 1)
+        g.vector.tensor_copy(T.ys[:, HW * h:HW * (h + 1)], T["ps%d" % h][:, 0:HW]).then_inc(T.sem["cp%d" % h], 1)
+        q.wait_ge(T.sem["cp%d" % h], 1)
+        q.dma_start(T.y[:, HW * h:HW * (h + 1)], T.ys[:, HW * h:HW * (h + 1)]).then_inc(T.sem["st%d" % h], 16)
+        q.wait_ge(T.sem["st%d" % h], 16)

@@ -13,12 +13,13 @@ SCRATCH = {
     "land1": ("sbuf", [P, TK], "bfloat16"),
     "land2": ("sbuf", [P, TK], "bfloat16"),
     "ys": ("sbuf", [P, TK], "bfloat16"),
-    "xd": ("dram", [P, TK], "bfloat16"),
-    "rd": ("dram", [P, TK], "bfloat16"),
+    "xh": ("dram", [NH, P, HW], "bfloat16"),
+    "rd": ("dram", [P, HW], "bfloat16"),
     "ps0": ("psum", [P, TK], "float32"),
     "ps1": ("psum", [P, TK], "float32"),
 }
-SEMAPHORES = ["ldd", "ldx", "ldw", "fed", "sent", "a0", "a1", "a2", "mm0", "mm1", "cp0", "cp1", "st0", "st1"]
+SEMAPHORES = ["ldd", "ldx", "ldw", "fed", "sent", "a0", "a1", "a2", "b0", "b1", "b2",
+              "mm0", "mm1", "cp0", "cp1", "st0", "st1"]
 
 _CACHE = {}
 
@@ -52,100 +53,106 @@ def _make_plan(T, topo):
     def where(c):
         return (topo.host(c), topo.chip(c))
 
-    direct, units = {}, []
+    units, home = [], {}
     for j in range(n):
+        by_chip = {}
         for r in range(n):
             if r != j and j in mask[r]:
-                if topo.may_write(cores[j], cores[r]):
-                    direct.setdefault(j, []).append(r)
+                if where(cores[r]) == where(cores[j]):
+                    home.setdefault(j, []).append(r)
                 else:
-                    units.append((j, r))
+                    by_chip.setdefault(where(cores[r]), []).append(r)
+        for chip in sorted(by_chip):
+            units.append((j, by_chip[chip]))
 
-    owners = []
-    for j, r in units:
+    owners = {}
+    for j in sorted(set(j for j, _ in units)):
         by_die = {}
         for c in world:
-            if where(c) == where(cores[j]) and T.rank_of(c) is None and topo.may_write(c, cores[r]):
+            if where(c) == where(cores[j]) and T.rank_of(c) is None and all(topo.may_write(c, d) for d in cores):
                 by_die.setdefault(topo.die(c), []).append(c)
-        owners.append(by_die)
+        owners[j] = {d: v for d, v in by_die.items() if len(v) >= NH}
 
-    base = {}
-    for j, rs in direct.items():
-        for r in rs:
-            if where(cores[j]) != where(cores[r]):
-                d = topo.die(cores[j])
-                for key in (("out", where(cores[j]), d), ("in", where(cores[r]), d)):
-                    base[key] = base.get(key, 0) + 1
-
+    options = []
+    for j, rs in units:
+        may = all(topo.may_write(cores[j], cores[r]) for r in rs)
+        options.append(([None] if may else []) + sorted(owners[j]))
     best, total = None, 1
-    for by_die in owners:
-        total *= len(by_die)
+    for o in options:
+        total *= len(o)
     for code in range(total):
-        load, count, pick, cross = dict(base), {}, [], 0
-        for (j, r), by_die in zip(units, owners):
-            dies = sorted(by_die)
-            d = dies[code % len(dies)]
-            code //= len(dies)
+        load, sends, pick, extra = {}, {}, [], 0
+        for (j, rs), o in zip(units, options):
+            d = o[code % len(o)]
+            code //= len(o)
             pick.append(d)
-            cross += d != topo.die(cores[j])
-            keys = [("mate", where(cores[j]), d)]
-            if not topo.mates(cores[j], cores[r]):
-                keys.append(("in", where(cores[r]), d))
+            die = topo.die(cores[j]) if d is None else d
+            plane = topo.same_plane(cores[j], cores[rs[0]])
+            keys = [("out" if plane else "mate", where(cores[j]), die)]
+            if not topo.mates(cores[j], cores[rs[0]]):
+                keys.append(("in", where(cores[rs[0]]), die))
             for key in keys:
-                load[key] = load.get(key, 0) + 1
-            key = (j, d, len(by_die[d]))
-            count[key] = count.get(key, 0) + 1
-        busy = list(load.values()) + [-(-v // key[2]) for key, v in count.items()]
-        score = (sorted(busy, reverse=True), cross)
+                load[key] = load.get(key, 0) + len(rs)
+            if d is not None:
+                sends[(j, d)] = sends.get((j, d), 0) + len(rs)
+                extra += o[0] is None
+        score = (max(load.values()), max(sends.values()) if sends else 0, sum(v * v for v in load.values()), extra)
         if best is None or score < best[0]:
             best = (score, pick)
 
-    relays, feeds, seen = {}, {}, {}
-    for (j, r), by_die, d in zip(units, owners, best[1] if best else []):
-        k = seen.get((j, d), 0)
-        seen[(j, d)] = k + 1
-        c = by_die[d][k % len(by_die[d])]
-        if c not in relays:
-            relays[c] = {"src": j, "dests": []}
-            feeds.setdefault(j, []).append((k, d != topo.die(cores[j]), c))
-        relays[c]["dests"].append(r)
-    feeds = {j: [c for _, _, c in sorted(v)] for j, v in feeds.items()}
+    direct, by_relay_die = {}, {}
+    for (j, rs), d in zip(units, best[1] if best else []):
+        if d is None:
+            direct.setdefault(j, []).extend(rs)
+        else:
+            by_relay_die.setdefault(j, {}).setdefault(d, []).extend(rs)
+
+    relays, feeds = {}, {}
+    for j, by_die in by_relay_die.items():
+        for h in range(NH):
+            for d in sorted(by_die, key=lambda d: d != topo.die(cores[j])):
+                c = owners[j][d][h]
+                relays[c] = {"src": j, "half": h, "dests": by_die[d]}
+                feeds.setdefault(j, []).append(c)
 
     count, late, calls = {}, {}, {}
-    for j in sorted(set(direct) | set(feeds)):
+    for j in sorted(set(direct) | set(feeds) | set(home)):
         src, first, second = cores[j], [], []
         hs = feeds.get(j, [])
         if hs:
             for c, m in zip(hs, _deal(_bits(topo.mask(src, hs[0])), len(hs), FEED_ENGINES)):
                 first.append((c, m))
                 relays[c]["fed"] = len(_bits(m))
-        away = [r for r in direct.get(j, []) if where(cores[r]) != where(src)]
-        home = [r for r in direct.get(j, []) if where(cores[r]) == where(src)]
+        away, near = direct.get(j, []), home.get(j, [])
         taken = _bits(topo.mask(src, cores[away[0]])) if away else []
         for rs, engines, hops in ((away, taken, 2),
-                                  (home, [e for e in _bits(topo.mask(src, cores[home[0]])) if e not in taken] if home else [], 1)):
+                                  (near, [e for e in _bits(topo.mask(src, cores[near[0]])) if e not in taken] if near else [], 1)):
             if rs:
                 for r, m in zip(rs, _deal(engines, len(rs), _pow2(len(engines) // len(rs)))):
                     second.append((r, m))
                     count[(r, j)], late[(r, j)] = len(_bits(m)), (hops, 0)
         calls[j] = (first, second)
+    halved = set()
     for c, job in relays.items():
         ds = job["dests"]
         engines = _bits(topo.mask(c, cores[ds[0]]))
+        for r in ds:
+            engines = [e for e in engines if e in _bits(topo.mask(c, cores[r]))]
         job["masks"] = _deal(engines, len(ds), _pow2(min(OUT_ENGINES, len(engines)) // len(ds)))
         for r, m in zip(ds, job["masks"]):
+            halved.add((r, job["src"]))
             count[(r, job["src"])], late[(r, job["src"])] = len(_bits(m)), (3, len(feeds[job["src"]]))
-    return {"relays": relays, "calls": calls, "count": count, "late": late}
+    return {"relays": relays, "calls": calls, "count": count, "late": late, "halved": halved}
 
 
-def _send(g, core, T, topo, src_ap, items):
+def _send(g, core, T, topo, items):
     trs = []
-    for dst, ap, sem, m in items:
+    for src_ap, dst, ap, sem, m in items:
         rid, pid = topo.addr(dst, core)
         trs.append(RemoteDMATransfer(dst_ids=[DstId(rid=rid, pnc=pid)], dma_engine_mask=m, remote_sem=sem,
                                      src=src_ap, dst=ap))
     g.remote_dma_fused(trs, local_sem=T.sem.sent)
-    return sum(len(_bits(m)) for _, _, _, m in items)
+    return sum(len(_bits(it[4])) for it in items)
 
 
 def rank_program(g, core, T, topo):
@@ -155,52 +162,62 @@ def rank_program(g, core, T, topo):
     cores, mask = list(T.cores), T.tables["MASK"]
     rank = T.rank_of(core)
 
-    def landing(r, j):
-        i = mask[r].index(j)
-        return cores[r], T["land%d" % i][:], T.sem["a%d" % i]
-
     if rank is None:
         job = plan["relays"].get(core)
         if job is None:
             return
+        h = job["half"]
         g.wait_ge(T.sem.fed, job["fed"])
-        left = _send(g, core, T, topo, T.rd[:], [landing(r, job["src"]) + (m,) for r, m in zip(job["dests"], job["masks"])])
+        items = []
+        for r, m in zip(job["dests"], job["masks"]):
+            i = mask[r].index(job["src"])
+            items.append((T.rd[:], cores[r], T["land%d" % i][:, HW * h:HW * (h + 1)], T.sem["ab"[h] + "%d" % i], m))
+        left = _send(g, core, T, topo, items)
         g.wait_ge(T.sem.sent, left)
         return
 
-    source = rank in plan["calls"]
-    if source:
-        g.sync.dma_start(T.xd[:], T.x[:]).then_inc(T.sem.ldd, 16)
-    if rank in mask[rank]:
+    first, second = plan["calls"].get(rank, ([], []))
+    if first:
+        for h, q in zip(range(NH), (g.sync, g.scalar)):
+            q.dma_start(T.xh[h], T.x[:, HW * h:HW * (h + 1)]).then_inc(T.sem.ldd, 16)
+    if second or rank in mask[rank]:
         g.sync.dma_start(T.xs[:], T.x[:]).then_inc(T.sem.ldx, 16)
-    (g.sync if source else g.scalar).dma_start(T.ws[:], T.w[:]).then_inc(T.sem.ldw, 16)
+    g.scalar.dma_start(T.ws[:], T.w[:]).then_inc(T.sem.ldw, 16)
 
-    if source:
-        first, second = plan["calls"][rank]
-        g.wait_ge(T.sem.ldd, 16)
-        left = 0
-        if first:
-            left += _send(g, core, T, topo, T.xd[:], [(c, T.rd[:], T.sem.fed, m) for c, m in first])
-        if second:
-            left += _send(g, core, T, topo, T.xd[:], [landing(r, rank) + (m,) for r, m in second])
+    left = 0
+    if first:
+        g.wait_ge(T.sem.ldd, 16 * NH)
+        left += _send(g, core, T, topo,
+                      [(T.xh[plan["relays"][c]["half"]], c, T.rd[:], T.sem.fed, m) for c, m in first])
+    if second:
+        g.wait_ge(T.sem.ldx, 16)
+        left += _send(g, core, T, topo,
+                      [(T.xs[:], cores[r], T["land%d" % mask[r].index(rank)][:], T.sem["a%d" % mask[r].index(rank)], m)
+                       for r, m in second])
+    if left:
         g.wait_ge(T.sem.sent, left)
 
     te = g.tensor
     te.wait_ge(T.sem.ldw, 16)
-    order = sorted(range(DEG), key=lambda i: plan["late"].get((rank, mask[rank][i]), (0, 0)))
-    for k, i in enumerate(order):
+    steps = []
+    for i in sorted(range(DEG), key=lambda i: plan["late"].get((rank, mask[rank][i]), (0, 0))):
         j = mask[rank][i]
         if j == rank:
-            te.wait_ge(T.sem.ldx, 16)
-            buf = T.xs
+            steps.append((T.sem.ldx, 16, i, T.xs, list(range(NH))))
+        elif (rank, j) in plan["halved"]:
+            for h in range(NH):
+                steps.append((T.sem["ab"[h] + "%d" % i], plan["count"][(rank, j)], i, T["land%d" % i], [h]))
         else:
-            _, _, sem = landing(rank, j)
-            te.wait_ge(sem, plan["count"][(rank, j)])
-            buf = T["land%d" % mask[rank].index(j)]
-        for h in range(NH):
+            steps.append((T.sem["a%d" % i], plan["count"][(rank, j)], i, T["land%d" % i], list(range(NH))))
+    todo = [sum(h in s[4] for s in steps) for h in range(NH)]
+    done = [0] * NH
+    for sem, cnt, i, buf, banks in steps:
+        te.wait_ge(sem, cnt)
+        for h in banks:
+            done[h] += 1
             mm = te.matmul(T["ps%d" % h][:, 0:HW], T.ws[:, P * i:P * (i + 1)], buf[:, HW * h:HW * (h + 1)],
-                           k == 0, k == DEG - 1)
-            if k == DEG - 1:
+                           done[h] == 1, done[h] == todo[h])
+            if done[h] == todo[h]:
                 mm.then_inc(T.sem["mm%d" % h], 1)
 
     for h, q in zip(range(NH), (g.sync, g.scalar)):

from concourse.bass import DstId, RemoteDMATransfer

P, TK, DEG = 128, 512, 3
NH = 2
HW = TK // NH
FEED_ENGINES = 4
OUT_ENGINES = 8

SCRATCH = {
    "xs": ("sbuf", [P, TK], "bfloat16"),
    "ws": ("sbuf", [P, DEG * P], "bfloat16"),
    "land0": ("sbuf", [P, TK], "bfloat16"),
    "land1": ("sbuf", [P, TK], "bfloat16"),
    "land2": ("sbuf", [P, TK], "bfloat16"),
    "ys": ("sbuf", [P, TK], "bfloat16"),
    "xh": ("dram", [NH, P, HW], "bfloat16"),
    "rd": ("dram", [P, HW], "bfloat16"),
    "ps0": ("psum", [P, TK], "float32"),
    "ps1": ("psum", [P, TK], "float32"),
}
SEMAPHORES = ["ldd", "ldx", "ldw", "fed", "sent", "a0", "a1", "a2", "b0", "b1", "b2",
              "mm0", "mm1", "cp0", "cp1", "st0", "st1"]

_CACHE = {}


def _bits(m):
    return [e for e in range(m.bit_length()) if (m >> e) & 1]


def _pow2(n):
    k = 1
    while 2 * k <= n:
        k *= 2
    return k


def _spread(engines, k):
    k = min(k, len(engines))
    return engines[::len(engines) // k][:k]


def _deal(engines, n, k):
    used = _spread(engines, n * k)
    return [sum(1 << e for e in used[t::n]) for t in range(n)]


def _make_plan(T, topo):
    cores, mask = list(T.cores), T.tables["MASK"]
    n = len(cores)
    world = range(topo.CORES_PER_HOST * (1 + max(topo.host(c) for c in cores)))

    def where(c):
        return (topo.host(c), topo.chip(c))

    units, home = [], {}
    for j in range(n):
        by_chip = {}
        for r in range(n):
            if r != j and j in mask[r]:
                if where(cores[r]) == where(cores[j]):
                    home.setdefault(j, []).append(r)
                else:
                    by_chip.setdefault(where(cores[r]), []).append(r)
        for chip in sorted(by_chip):
            units.append((j, by_chip[chip]))

    owners = {}
    for j in sorted(set(j for j, _ in units)):
        by_die = {}
        for c in world:
            if where(c) == where(cores[j]) and T.rank_of(c) is None and all(topo.may_write(c, d) for d in cores):
                by_die.setdefault(topo.die(c), []).append(c)
        owners[j] = {d: v for d, v in by_die.items() if len(v) >= NH}

    options = []
    for j, rs in units:
        may = all(topo.may_write(cores[j], cores[r]) for r in rs)
        options.append(([None] if may else []) + sorted(owners[j]))
    best, total = None, 1
    for o in options:
        total *= len(o)
    for code in range(total):
        load, sends, pick, extra = {}, {}, [], 0
        for (j, rs), o in zip(units, options):
            d = o[code % len(o)]
            code //= len(o)
            pick.append(d)
            die = topo.die(cores[j]) if d is None else d
            plane = topo.same_plane(cores[j], cores[rs[0]])
            keys = [("out" if plane else "mate", where(cores[j]), die)]
            if not topo.mates(cores[j], cores[rs[0]]):
                keys.append(("in", where(cores[rs[0]]), die))
            for key in keys:
                load[key] = load.get(key, 0) + len(rs)
            if d is not None:
                sends[(j, d)] = sends.get((j, d), 0) + len(rs)
                extra += o[0] is None
        score = (max(load.values()), max(sends.values()) if sends else 0, sum(v * v for v in load.values()), extra)
        if best is None or score < best[0]:
            best = (score, pick)

    direct, by_relay_die = {}, {}
    for (j, rs), d in zip(units, best[1] if best else []):
        if d is None:
            direct.setdefault(j, []).extend(rs)
        else:
            by_relay_die.setdefault(j, {}).setdefault(d, []).extend(rs)

    relays, feeds = {}, {}
    for j, by_die in by_relay_die.items():
        for h in range(NH):
            for d in sorted(by_die, key=lambda d: d != topo.die(cores[j])):
                c = owners[j][d][h]
                relays[c] = {"src": j, "half": h, "dests": by_die[d]}
                feeds.setdefault(j, []).append(c)

    count, late, calls = {}, {}, {}
    for j in sorted(set(direct) | set(feeds) | set(home)):
        src, first, second = cores[j], [], []
        hs = feeds.get(j, [])
        if hs:
            for c, m in zip(hs, _deal(_bits(topo.mask(src, hs[0])), len(hs), FEED_ENGINES)):
                first.append((c, m))
                relays[c]["fed"] = len(_bits(m))
        away, near = direct.get(j, []), home.get(j, [])
        taken = _bits(topo.mask(src, cores[away[0]])) if away else []
        for rs, engines, hops in ((away, taken, 2),
                                  (near, [e for e in _bits(topo.mask(src, cores[near[0]])) if e not in taken] if near else [], 1)):
            if rs:
                for r, m in zip(rs, _deal(engines, len(rs), _pow2(len(engines) // len(rs)))):
                    second.append((r, m))
                    count[(r, j)], late[(r, j)] = len(_bits(m)), (hops, 0)
        calls[j] = (first, second)
    halved = set()
    for c, job in relays.items():
        ds = job["dests"]
        engines = _bits(topo.mask(c, cores[ds[0]]))
        for r in ds:
            engines = [e for e in engines if e in _bits(topo.mask(c, cores[r]))]
        job["masks"] = _deal(engines, len(ds), _pow2(min(OUT_ENGINES, len(engines)) // len(ds)))
        for r, m in zip(ds, job["masks"]):
            halved.add((r, job["src"]))
            count[(r, job["src"])], late[(r, job["src"])] = len(_bits(m)), (3, len(feeds[job["src"]]))
    return {"relays": relays, "calls": calls, "count": count, "late": late, "halved": halved}


def _send(g, core, T, topo, items):
    trs = []
    for src_ap, dst, ap, sem, m in items:
        rid, pid = topo.addr(dst, core)
        trs.append(RemoteDMATransfer(dst_ids=[DstId(rid=rid, pnc=pid)], dma_engine_mask=m, remote_sem=sem,
                                     src=src_ap, dst=ap))
    g.remote_dma_fused(trs, local_sem=T.sem.sent)
    return sum(len(_bits(it[4])) for it in items)


def rank_program(g, core, T, topo):
    if "plan" not in _CACHE:
        _CACHE["plan"] = _make_plan(T, topo)
    plan = _CACHE["plan"]
    cores, mask = list(T.cores), T.tables["MASK"]
    rank = T.rank_of(core)

    if rank is None:
        job = plan["relays"].get(core)
        if job is None:
            return
        h = job["half"]
        g.wait_ge(T.sem.fed, job["fed"])
        items = []
        for r, m in zip(job["dests"], job["masks"]):
            i = mask[r].index(job["src"])
            items.append((T.rd[:], cores[r], T["land%d" % i][:, HW * h:HW * (h + 1)], T.sem["ab"[h] + "%d" % i], m))
        left = _send(g, core, T, topo, items)
        g.wait_ge(T.sem.sent, left)
        return

    first, second = plan["calls"].get(rank, ([], []))
    if first:
        for h, q in zip(range(NH), (g.sync, g.scalar)):
            q.dma_start(T.xh[h], T.x[:, HW * h:HW * (h + 1)]).then_inc(T.sem.ldd, 16)
    if second or rank in mask[rank]:
        g.sync.dma_start(T.xs[:], T.x[:]).then_inc(T.sem.ldx, 16)
    g.scalar.dma_start(T.ws[:], T.w[:]).then_inc(T.sem.ldw, 16)

    left = 0
    if first:
        g.wait_ge(T.sem.ldd, 16 * NH)
        left += _send(g, core, T, topo,
                      [(T.xh[plan["relays"][c]["half"]], c, T.rd[:], T.sem.fed, m) for c, m in first])
    if second:
        g.wait_ge(T.sem.ldx, 16)
        left += _send(g, core, T, topo,
                      [(T.xs[:], cores[r], T["land%d" % mask[r].index(rank)][:], T.sem["a%d" % mask[r].index(rank)], m)
                       for r, m in second])
    if left:
        g.wait_ge(T.sem.sent, left)

    te = g.tensor
    te.wait_ge(T.sem.ldw, 16)
    steps = []
    for i in sorted(range(DEG), key=lambda i: plan["late"].get((rank, mask[rank][i]), (0, 0))):
        j = mask[rank][i]
        if j == rank:
            steps.append((T.sem.ldx, 16, i, T.xs, list(range(NH))))
        elif (rank, j) in plan["halved"]:
            for h in range(NH):
                steps.append((T.sem["ab"[h] + "%d" % i], plan["count"][(rank, j)], i, T["land%d" % i], [h]))
        else:
            steps.append((T.sem["a%d" % i], plan["count"][(rank, j)], i, T["land%d" % i], list(range(NH))))
    todo = [sum(h in s[4] for s in steps) for h in range(NH)]
    done = [0] * NH
    for sem, cnt, i, buf, banks in steps:
        te.wait_ge(sem, cnt)
        for h in banks:
            done[h] += 1
            mm = te.matmul(T["ps%d" % h][:, 0:HW], T.ws[:, P * i:P * (i + 1)], buf[:, HW * h:HW * (h + 1)],
                           done[h] == 1, done[h] == todo[h])
            if done[h] == todo[h]:
                mm.then_inc(T.sem["mm%d" % h], 1)

    for h, q in zip(range(NH), (g.sync, g.scalar)):
        g.vector.wait_ge(T.sem["mm%d" % h], 1)
        g.vector.tensor_copy(T.ys[:, HW * h:HW * (h + 1)], T["ps%d" % h][:, 0:HW]).then_inc(T.sem["cp%d" % h], 1)
        q.wait_ge(T.sem["cp%d" % h], 1)
        q.dma_start(T.y[:, HW * h:HW * (h + 1)], T.ys[:, HW * h:HW * (h + 1)]).then_inc(T.sem["st%d" % h], 16)
        q.wait_ge(T.sem["st%d" % h], 16)
